import numpy as np
CORES = [5,21,45,77,85,101,109,125,133,141,189,213]
N = 12
R, B, K = 4096, 256, 8
T = B * K
CAPP = 512
def entries(a): return a.T.reshape(-1)
def pack(v, P): return np.ascontiguousarray(np.asarray(v, np.int32).reshape(-1, P).T)
def lists(rng, how):
    O = np.stack([rng.permutation(np.repeat(np.arange(N), CAPP))[:T] for r in range(N)])
    if how in ("full", "none"):
        h = 0 if how == "none" else int(rng.integers(N))
        O = np.stack([rng.permutation(np.repeat(np.append(rng.permutation(np.delete(np.arange(N), h))[:T // CAPP - 1], h), CAPP)) for r in range(N)])
    I = R * O + rng.integers(0, R, (N, T))
    if how == "alike": I = R * O + I[:, :1] % R
    if how == "edge": I = np.stack([rng.permutation(R * (np.arange(T) % N) + (R - 1) * (np.arange(T) // N % 2)) for r in range(N)])
    if how == "twice":
        G = np.sort(I, axis=1).reshape(N, B, K); G = np.where(G[:, :, :1] // R == G[:, :, -1:] // R, G[:, :, :1], G)
        G[1::2] = np.stack([g[rng.permutation(B)] for g in G[1::2]]); I = G.reshape(N, T)
    if how == "none":
        I[(O > 0) & (O == O.max(axis=1, keepdims=True))] = -1
        I[::2] = np.sort(I[::2], axis=1); I[int(rng.integers(N))] = -1
    return {"col": np.stack([pack(i, 16) for i in I])}
def setup_inputs(rng):
    return wt0(dict({"tab": rng.standard_normal((N, 128, R), dtype=np.float32), "wt": rng.standard_normal((N, 16, T // 16), dtype=np.float32)}, **lists(rng, "uniform")))
def setup_inputs_alike(rng):
    d = setup_inputs(rng); d.update(lists(rng, "alike"))
    for k in ("tab",): d[k] = (d[k].astype(np.float32) * 1024.0).astype(d[k].dtype)
    return wt0(d)
def setup_inputs_edge(rng):
    d = setup_inputs(rng); d.update(lists(rng, "edge"))
    for k in ("tab",): d[k] = (d[k].astype(np.float32) * (1 / 1024.0)).astype(d[k].dtype)
    return wt0(d)
def setup_inputs_full(rng):
    d = setup_inputs(rng); d.update(lists(rng, "full"))
    return wt0(d)
def setup_inputs_none(rng):
    d = setup_inputs(rng); d.update(lists(rng, "none"))
    return wt0(d)
def setup_inputs_twice(rng):
    d = setup_inputs(rng); d.update(lists(rng, "twice"))
    return wt0(d)
def wt0(d): d["wt"] = d["wt"] * (d["col"] >= 0); return d
def check_inputs(x):
    bad = []
    if x["col"].min() < -1 or x["col"].max() >= N * R: bad.append("col out of range")
    if (x["wt"][x["col"] < 0] != 0).any(): bad.append("a void term with a weight")
    if max(int(np.bincount(entries(a)[entries(a) >= 0] // R, minlength=N).max()) for a in x["col"]) > CAPP: bad.append("more than CAPP entries of a list point into one rank's part")
    return bad
def reference(tab, wt, col):
    A = np.concatenate(list(tab), axis=1).astype(np.float64)
    return {"y": np.stack([(A[:, np.maximum(entries(col[r]), 0)] * entries(wt[r]).astype(np.float64)[None, :]).reshape(128, B, K).sum(axis=2) for r in range(N)]).astype(np.float32)}

from concourse.bass import DstId, RemoteDMATransfer
from concourse.mybir import AluOpType as A, ActivationFunctionType as F

N, ROWS, Z, CH, NC = 12, 4096, 4, 512, 8
SCRATCH = {}
for _dt, _names in {
        "float32": "tabs 4104 land 3072 gq 2048 kcol 1 kmodf 1 ind 16 ident 128 pa 1024 ta 512 uu 512 ysb 256 part1 256 part2 256 "
                   "part3 256 w30 128 w31 128 w32 128 w33 128 r1 128 r2 128 posr0 128 posr1 128 posr2 128 posr3 128",
        "uint16": "off0 128 off1 128 off2 128 off3 128",
        "int32": "colv0 16 colv1 16 colv2 16 colv3 16 kint 1 kmod 1",
        "bfloat16": "iot 128 ones 128 selw 2048 h1 128 h2 128 hs0 128 hs1 128 hs2 128 hs3 128"}.items():
    _w = _names.split()
    SCRATCH.update({_w[i]: ("sbuf", [128, int(_w[i + 1])], _dt) for i in range(0, len(_w), 2)})
SCRATCH.update({"lcs": ("dram", [128, 16], "int32"), "lws": ("dram", [128, 16], "float32"),
                "rc": ("dram", [128, 16], "int32"), "rw": ("dram", [128, 16], "float32"),
                "lc": ("dram", [3, 128, 16], "int32"), "lw": ("dram", [3, 128, 16], "float32"),
                "wb0": ("psum", [128, 1024], "float32"), "wb1": ("psum", [128, 1024], "float32")})
SCRATCH.update({k: ("psum", [128, 512], "float32") for k in ("pb0", "pb1", "tb", "pso")})
SEMAPHORES = (["dl", "dy", "kc", "v", "pe", "s", "rl", "sent", "tcx", "tc0", "tc1"] + ["dt%d" % i for i in range(NC)]
              + ["ls%d" % i for i in range(3)] + ["du%d" % i for i in range(4)] + ["arr%d" % i for i in range(1, N)])


def engines(mask):
    return [i for i in range(16) if mask >> i & 1]


def to_mask(es):
    return sum(1 << i for i in es)


def rank_program(g, core, T, topo):
    R = T.cores

    def chipmates(c):
        return [d for d in range(256) if topo.host(d) == topo.host(c) and topo.chip(d) == topo.chip(c)]

    def helpers(c):
        h = [d for d in chipmates(c) if d != c and all(topo.may_write(d, r) for r in R)]
        return ([d for d in h if topo.die(d) != topo.die(c)] + [d for d in h if topo.die(d) == topo.die(c)])[:4]

    mine = [r for r in R if r in chipmates(core)]
    if not mine:
        return
    P = mine[0]
    X = helpers(P)
    if core != P and core not in X:
        return
    plane = [r for r in R if r == P or topo.may_write(P, r)]
    cross = [r for r in R if r not in plane]
    n = len(plane)
    a = plane.index(P)
    S = T.sem
    V, SC, PE, SY = g.vector, g.scalar, g.tensor, g.sync
    cnt = {}
    own_units = [("s", t) for t in (1, 2, 3)]
    help_units = [[("x", 0), ("s", 4)], [("x", 1), ("s", 5)], [("x", 2), ("x", 3)], [("x", 4), ("x", 5)]]

    def inc(ins, name, k=1):
        ins.then_inc(S[name], k)
        cnt[name] = cnt.get(name, 0) + k
        return cnt[name]

    far = [r for r in plane if r != P][0]
    off_es = engines(topo.mask(P, far))
    all_es = engines(topo.mask(P, X[0]))
    lo, hi = off_es[:len(off_es) // 2], off_es[len(off_es) // 2:]

    def tr(dsts, src, sem, es):
        ad = [topo.addr(d, core) for d, _ in dsts]
        cnt["sent"] = cnt.get("sent", 0) + len(es)
        return RemoteDMATransfer(dst_ids=[DstId(rid=r, pnc=p) for r, p in ad], dma_engine_mask=to_mask(es),
                                 remote_sem=S[sem], srcs=[src], dsts=[o for _, o in dsts])

    def fused(trs):
        g.remote_dma_fused(trs, local_sem=S.sent)

    def chunk(c):
        return T.tabs[:, Z + c * CH:Z + (c + 1) * CH]

    def place(kind, t):
        if (kind, t) in own_units:
            return 0, own_units.index((kind, t))
        i = [j for j in range(4) if (kind, t) in help_units[j]][0]
        return i + 1, help_units[i].index((kind, t))

    def lists(steps, src_c, src_w):
        by = {}
        for kind, t in steps:
            o = (plane if kind == "s" else cross)[(a - t) % n]
            i, slot = place(kind, t)
            by.setdefault(slot, []).append(o if i == 0 else helpers(o)[i - 1])
        for slot in sorted(by):
            fused([tr([(d, T.lc[slot]) for d in by[slot]], src_c, "ls%d" % slot, lo),
                   tr([(d, T.lw[slot]) for d in by[slot]], src_w, "ls%d" % slot, hi)])

    def ts(out, in0, s1, op0, s2=None, op1=None):
        if op1 is None:
            return inc(V.tensor_scalar(out=out, in0=in0, scalar1=s1, scalar2=None, op0=op0), "v")
        return inc(V.tensor_scalar(out=out, in0=in0, scalar1=s1, scalar2=s2, op0=op0, op1=op1), "v")

    def tt(out, x, y, op):
        return inc(V.tensor_tensor(out=out, in0=x, in1=y, op=op), "v")

    def cp(out, in_):
        return inc(V.tensor_copy(out, in_), "v")

    def vwait(k=None):
        V.wait_ge(S.v, cnt["v"] if k is None else k)

    units = ([("self", 0)] + own_units) if core == P else help_units[X.index(core)]
    U = len(units)
    H = 2 * U

    for u in range(U):
        inc(V.memset(T["w3%d" % u][:], 0.0), "v")
    k_w3 = cnt["v"]
    inc(V.memset(T.tabs[:, 0:Z], 0.0), "v")
    inc(V.memset(T.tabs[:, Z + ROWS:2 * Z + ROWS], 0.0), "v")
    for u in range(U):
        inc(V.memset(T["hs%d" % u][:], 0.0), "v")
    inc(V.memset(T.ones[:], 1.0), "v")

    def load_unit(q, u, c_src, w_src):
        inc(q.dma_start(T["colv%d" % u][:], c_src), "du%d" % u, 16)
        for p in (0, 32, 64):
            inc(q.dma_start(T["w3%d" % u][p:p + 16, :], w_src), "du%d" % u, 16)

    if core == P:
        inc(SY.dma_start(T.lcs[:], T.col[:]), "dl", 16)
        inc(SC.dma_start(T.lws[:], T.wt[:]), "dl", 16)
        for c in range(NC):
            inc((SY if c % 2 == 0 else SC).dma_start(chunk(c), T.tab[:, c * CH:(c + 1) * CH]), "dt%d" % c, 16)
            if c == 1:
                SC.wait_ge(S.v, k_w3)
                load_unit(SC, 0, T.col[:], T.wt[:])
    SY.wait_ge(S.v, k_w3)
    for slot in range(len(own_units) if core == P else U):
        SY.wait_ge(S["ls%d" % slot], len(off_es))
        load_unit(SY, slot + (1 if core == P else 0), T.lc[slot], T.lw[slot])

    inc(g.iota(T.kint[:], pattern=[[0, 1]], base=0, channel_multiplier=1), "kc")
    inc(g.iota(T.iot[:], pattern=[[1, 128]], base=0, channel_multiplier=0, allow_small_or_imprecise_dtypes=True), "kc")
    if core == P:
        for c in range(NC):
            g.wait_ge(S["dt%d" % c], 16)
            fused([tr([(X[c % 4], chunk(c))], chunk(c), "tc%d" % (c // 4), all_es)])
            if c == 1:
                g.wait_ge(S.dl, 32)
                fused([tr([(x, T.rc[:]) for x in X], T.lcs[:], "rl", lo),
                       tr([(x, T.rw[:]) for x in X], T.lws[:], "rl", hi)])
                lists([("s", t) for t in range(1, n)], T.lcs[:], T.lws[:])
    else:
        me = X.index(core)
        peers = [x for x in X if x != core]
        g.wait_ge(S.tc0, len(all_es))
        fused([tr([(x, chunk(me)) for x in peers], chunk(me), "tcx", all_es)])
        g.wait_ge(S.rl, len(off_es))
        lists([ut for ut in help_units[me] if ut[0] == "x"], T.rc[:], T.rw[:])
        g.wait_ge(S.tc1, len(all_es))
        fused([tr([(x, chunk(4 + me)) for x in peers], chunk(4 + me), "tcx", all_es)])

    V.wait_ge(S.kc, 2)
    ts(T.kmod[:], T.kint[:], 31, A.bitwise_and)
    cp(T.kcol[:], T.kint[:])
    vwait()
    cp(T.kmodf[:], T.kmod[:])
    ts(T.ident[:], T.iot[:], T.kcol[:, 0:1], A.is_equal)
    vwait()
    ts(T.ind[:], T.iot[:, 0:16], T.kmodf[:, 0:1], A.is_equal)
    vwait()
    for r in range(16):
        ts(T.selw[:, 128 * r:128 * r + 128], T.ones[:], T.ind[:, r:r + 1], A.mult)
    k_const = cnt["v"]

    base = ROWS * T.rank_of(P)
    k_pos, k_hs, k_off, k_m, k_out = {}, {}, {}, {}, {}

    def prep(u):
        cv, w3, hs = T["colv%d" % u], T["w3%d" % u], T["hs%d" % u]
        V.wait_ge(S["du%d" % u], 64)
        for i in range(8):
            k_pos[u] = ts(T["posr%d" % u][:, 16 * i:16 * i + 16], cv[:], float(Z - base), A.add, float(Z + ROWS), A.min)
        vwait()
        cp(T.h1[0:80, :], w3[0:80, :])
        cp(hs[0:16, :], w3[0:16, :])
        vwait()
        tt(T.r1[0:80, :], w3[0:80, :], T.h1[0:80, :], A.subtract)
        vwait()
        cp(T.h2[0:80, :], T.r1[0:80, :])
        cp(hs[32:48, :], T.r1[32:48, :])
        vwait()
        tt(T.r2[0:80, :], T.r1[0:80, :], T.h2[0:80, :], A.subtract)
        vwait()
        k_hs[u] = cp(hs[64:80, :], T.r2[64:80, :])
        V.wait_ge(S.pe, 3 * u + 1)
        k_off[u] = cp(T["off%d" % u][:], T.pso[:, 0:128])

    def product(h):
        b, w = (h % 2) * 512, T["wb%d" % (h % 2)]
        V.wait_ge(S.s, h + 1)
        V.wait_ge(S.pe, 3 * (h // 2) + 2 + h % 2)
        q = 2 * b
        tt(T.pa[:, b:b + 512], T.gq[:, q:q + 512], w[:, 0:512], A.mult)
        k_m[h] = tt(T["pb%d" % (h % 2)][:], T.gq[:, q + 512:q + 1024], w[:, 512:1024], A.mult)

    kl = {}

    def level1(h):
        vwait(k_m[h])
        b, c = (h % 2) * 512, (h % 2) * 256
        pb = T["pb%d" % (h % 2)]
        tt(T.ta[:, c:c + 256], T.pa[:, b:b + 256], pb[:, 0:256], A.add)
        kl[1, h] = tt(T.tb[:, c:c + 256], T.pa[:, b + 256:b + 512], pb[:, 256:512], A.add)

    def level2(h):
        vwait(kl[1, h])
        c = (h % 2) * 256
        kl[2, h] = tt(T.uu[:, c:c + 256], T.ta[:, c:c + 256], T.tb[:, c:c + 256], A.add)

    def out_of(u):
        if core == P:
            return T.land[:, 0:256] if u == 0 else T["part%d" % u][:, 0:256]
        return T["part%d" % (u + 1)][:, 0:256]

    def level3(h):
        vwait(kl[2, h])
        c, o = (h % 2) * 256, (h % 2) * 128
        d = T.land if core == P and h < 2 else T["part%d" % (h // 2 + (0 if core == P else 1))]
        k_out[h] = tt(d[:, o:o + 128], T.uu[:, c:c + 128], T.uu[:, c + 128:c + 256], A.add)

    prep(0)
    if core != P:
        for u in range(1, U):
            prep(u)
    for h in range(H):
        product(h)
        if h:
            level2(h - 1)
        level1(h)
        if h:
            level3(h - 1)
        if core == P and h % 2 == 0 and h // 2 + 1 < U:
            prep(h // 2 + 1)
    level2(H - 1)
    level3(H - 1)

    PE.wait_ge(S.v, k_const)
    for u in range(U):
        PE.wait_ge(S.v, max(k_pos[u], k_off[u - 1] if u else 0))
        inc(PE.matmul(T.pso[:, 0:128], T["posr%d" % u][:], T.ident[:], True, True), "pe")
        PE.wait_ge(S.v, k_hs[u])
        for hh in range(2):
            h = 2 * u + hh
            if h >= 2:
                PE.wait_ge(S.v, k_m[h - 2])
            for k in range(8):
                r = 8 * hh + k
                m = PE.matmul(T["wb%d" % hh][:, 128 * k:128 * k + 128], T.selw[0:80, 128 * r:128 * r + 128],
                              T["hs%d" % u][0:80, :], True, True)
            inc(m, "pe")

    if core == P:
        for c in range(NC):
            SC.wait_ge(S["dt%d" % c], 16)
    else:
        SC.wait_ge(S.tc0, len(all_es))
        SC.wait_ge(S.tc1, len(all_es))
        SC.wait_ge(S.tcx, 6 * len(all_es))
    for h in range(H):
        u, hh = h // 2, h % 2
        SC.wait_ge(S.v, max(k_off[u], k_m[h - 2] if h >= 2 else 0))
        inc(SC.activation(T.gq[:, 1024 * hh:1024 * hh + 1024],
                          T.tabs[:, 0:2 * Z + ROWS].indirect(T["off%d" % u][:, 64 * hh:64 * hh + 64]), F.Copy), "s")

    for u in range(U):
        kind, t = units[u]
        if kind == "self":
            continue
        d = (plane if kind == "s" else cross)[(a + t) % n]
        blk = t if kind == "s" else n + t
        g.wait_ge(S.v, k_out[2 * u + 1])
        fused([tr([(d, T.land[:, 256 * blk:256 * blk + 256])], out_of(u), "arr%d" % blk, off_es)])

    if core == P:
        order = [1, 2, 3] + [n, n + 1, n + 2, n + 4] + [4, 5] + [n + 3, n + 5]
        acc = T.tb[:, 0:256]
        vwait()
        for i, blk in enumerate(order):
            V.wait_ge(S["arr%d" % blk], len(off_es))
            x = T.land[:, 256 * blk:256 * blk + 256]
            if i == 0:
                tt(acc, x, T.land[:, 0:256], A.add)
            elif i < len(order) - 1:
                tt(acc, x, acc, A.add)
            else:
                for hh in range(2):
                    b = 128 * hh
                    tt(T.ysb[:, hh:256:2], T.land[:, 256 * blk + b:256 * blk + b + 128], T.tb[:, b:b + 128], A.add)
            vwait()
        SY.wait_ge(S.v, cnt["v"])
        inc(SY.dma_start(T.y[:], T.ysb[:]), "dy", 16)
        SY.wait_ge(S.dy, 16)
    else:
        V.wait_ge(S.v, cnt["v"])
    g.wait_ge(S.sent, cnt["sent"])
